import numpy as np
import ml_dtypes


def mxq(x, axis, fmt="e4m3"):
    dtype, down = {"e4m3": (ml_dtypes.float8_e4m3fn, 7), "e5m2": (ml_dtypes.float8_e5m2, 14)}[fmt]
    v = np.moveaxis(np.asarray(x, np.float32).astype(ml_dtypes.bfloat16).astype(np.float64), axis, -1)
    blocks = v.reshape(v.shape[:-1] + (-1, 32))
    amax = np.abs(blocks).max(-1, keepdims=True)
    byte = np.maximum(np.where(amax > 0, np.frexp(amax)[1] - 1 + 127, 0) - down, 1)
    scale = np.exp2(byte - 127.0)
    codes = (blocks / scale).astype(np.float32).astype(dtype).astype(np.float64)
    return np.moveaxis((codes * scale).reshape(v.shape), -1, axis)


WIDE = False


def mx_kscale(k):
    if not WIDE:
        return np.ones(k)
    levels = np.array([10, -10, 5, -5, 0])
    if k % 512:
        return np.exp2(np.random.permutation(np.resize(levels, k // 32))).repeat(32)
    a = np.empty((k // 512, 16))
    for p in range(k // 512):
        a[p, :8] = np.random.permutation(np.resize(levels, 8))
        for g in range(8):
            far = levels[np.abs(levels - a[p, g]) >= 10]
            a[p, g + 8] = far[np.random.randint(len(far))]
    return np.exp2(a.ravel()).repeat(32)


def f64(x):
    return np.asarray(x).astype(np.float64)


def striped(idx):
    return np.tile(idx.reshape(-1, 16).T, (8, 1)).astype(np.uint16)


def unstriped(offs):
    return offs[:16].T.reshape(-1).astype(np.int64)


E2M1 = np.array([0.0, 0.5, 1.0, 1.5, 2.0, 3.0, 4.0, 6.0, -0.0, -0.5, -1.0, -1.5, -2.0, -3.0, -4.0, -6.0])


def pack_weight(w, fmt):
    k, n = w.shape
    w = f64(np.asarray(w, np.float32).astype(ml_dtypes.bfloat16)).reshape(k // 32, 32, n)
    amax = np.abs(w).max(1)
    if fmt == "e4m3":
        byte = np.frexp(amax)[1] - 1 + 127 - 7
    else:
        mant, ex = np.frexp(amax / 6.0)
        byte = np.where(mant > 0.5, ex, ex - 1) + 127
    byte = np.clip(np.where(amax > 0, byte, 1), 1, 254)
    scaled = (w * np.exp2(127.0 - byte)[:, None, :]).reshape(k, n).astype(np.float32)
    by_word = np.ascontiguousarray(scaled.reshape(k // 512, 128, 4, n).transpose(0, 1, 3, 2))
    if fmt == "e4m3":
        words = by_word.astype(ml_dtypes.float8_e4m3fn).view(np.uint8)
    else:
        c = by_word.astype(ml_dtypes.float4_e2m1fn).view(np.uint8) & 0xF
        words = (c[..., 0::2] | (c[..., 1::2] << 4)).reshape(k // 512, 128, 2 * n)
    return np.ascontiguousarray(words), np.ascontiguousarray(byte.astype(np.uint8).reshape(k // 512, 16, n))


def unpack_weight(words, scales, fmt):
    g, _, n = scales.shape
    words = np.ascontiguousarray(words).reshape(g, 128, n, -1)
    if fmt == "e4m3":
        vals = words.view(ml_dtypes.float8_e4m3fn).astype(np.float64)
    else:
        nib = np.empty((g, 128, n, 4), np.uint8)
        nib[..., 0::2] = words & 0xF
        nib[..., 1::2] = words >> 4
        vals = E2M1[nib]
    vals = vals * np.repeat(np.exp2(scales.astype(np.float64) - 127.0), 8, axis=1)[..., None]
    return vals.transpose(0, 1, 3, 2).reshape(g * 512, n)


def relu(v):
    return np.maximum(v, 0.0)


K, T, E, C, N = 1536, 1024, 12, 128, 256
R = 2


def by_expert(wq, xq):
    return np.concatenate([wq[e].T @ xq[:, e * C:(e + 1) * C] for e in range(E)], axis=1)


def setup_inputs():
    n = np.random.standard_normal
    s = mx_kscale(K)[:, None]
    slot_token = np.concatenate([r * (T // R) + np.random.permutation(T // R)[:C // R] for e in range(E) for r in range(R)])
    w = [pack_weight(m, "e2m1") for m in n((E, K, N)) / np.sqrt(K) / s[None]]
    return {
        "xT": (n((K, T)) * s).astype(np.float32),
        "w_words": np.stack([m[0] for m in w]),
        "w_scales": np.stack([m[1] for m in w]),
        "b": (0.3 * n((N, E))).astype(np.float32),
        "offs": striped(slot_token),
    }


def reference(xT, w_words, w_scales, b, offs):
    idx = unstriped(offs)
    w = np.stack([unpack_weight(w_words[e], w_scales[e], "e2m1") for e in range(E)])
    xq = mxq(f64(xT)[:, idx], 0, "e4m3")
    y = by_expert(w, xq)
    y = relu(y + np.repeat(f64(b), C, axis=1))
    return y.reshape(N, E, R, C // R).transpose(0, 2, 1, 3).reshape(N, E * C)

@@ -1,0 +1,141 @@
+import concourse.mybir as mybir
+
+FLOPS = 2 * 1536 * 1536 * 256
+
+K, T, E, C, N = 1536, 1024, 12, 128, 256
+P = 128
+PASSES = 3
+S = E * C
+F32 = mybir.dt.float32
+BF16 = mybir.dt.bfloat16
+I32 = mybir.dt.int32
+U32 = mybir.dt.uint32
+U16 = mybir.dt.uint16
+U8 = mybir.dt.uint8
+FP8X4 = mybir.dt.float8_e4m3fn_x4
+FP4X4 = mybir.dt.float4_e2m1fn_x4
+RELU = mybir.ActivationFunctionType.Relu
+
+CHUNKS = [(0, 0, 512, 288), (0, 512, 256, 144), (0, 768, 256, 144), (1, 0, 512, 0), (1, 512, 512, 0), (2, 0, 512, 0), (2, 512, 512, 192)]
+WORDS = [(0, 0, 0, 512), (0, 1, 0, 512), (0, 2, 0, 512), (1, 0, 0, 512), (1, 1, 0, 512), (2, 0, 0, 512), (2, 1, 0, 512), (1, 2, 0, 512), (2, 2, 0, 256), (2, 2, 256, 256)]
+LATE = [(1, 2)]
+BLOCKS = [4,4,4]
+STARTS = [sum(BLOCKS[:k]) for k in range(len(BLOCKS))]
+STORE_CUTS = [4,4,2,2]
+GATE = [4,5,6]
+LEAD = 4
+
+
+def tile_moe_eps_lin_relu_kernel(tc, xT, w_words, w_scales, b, offs, out):
+    nc = tc.nc
+    with (
+        tc.tile_pool(name="held", bufs=1) as held,
+        tc.psum_pool(name="psum", bufs=8) as psum,
+    ):
+        offsets = held.tile([P, S // 16], U16, name="offsets")
+        bias = held.tile([P, 2, E], F32, name="bias")
+        ws = held.tile([P, E * PASSES, N], U8, name="ws", align_bytes=64)
+        plane = held.tile([P, T], U8, name="plane", align_bytes=64)
+        codes = [held.tile([P, T], U32, name=f"codes{a}", align_bytes=64) for a in range(PASSES)]
+        ot = held.tile([P, 2, 2, E, 64], F32, name="ot", align_bytes=64)
+        block_of = [k for k, n in enumerate(BLOCKS) for i in range(n)]
+        sp = [
+            [held.tile([P, n * C], U8, name=f"sp{k}_{a}", align_bytes=64) for a in range(PASSES)] for k, n in enumerate(BLOCKS)
+        ]
+        warm = held.tile([P, 1], F32, name="warm")
+        nc.gpsimd.memset(warm[:], 0)
+        nc.scalar.activation(out=warm[:], in_=warm[:], func=RELU)
+        nc.gpsimd.memset(plane[:].bitcast(I32), 0)
+        nc.gpsimd.memset(ws[:].rearrange("p g n -> p (g n)").bitcast(I32), 0)
+        for k in range(len(BLOCKS)):
+            for a in (1, 2):
+                nc.gpsimd.memset(sp[k][a][:].bitcast(I32), 0)
+
+        raw = []
+        for i, (a, c0, w, v) in enumerate(CHUNKS):
+            r = held.tile([P, 4, w], F32, name=f"raw{i}", align_bytes=64)
+            nc.sync.dma_start(out=r[:], in_=xT[512 * a : 512 * a + 512, c0 : c0 + w].rearrange("(p j) w -> p j w", j=4))
+            raw.append(r)
+            if i == 1:
+                nc.sync.dma_start(offsets[:], offs)
+                nc.sync.dma_start(out=bias[:], in_=b.rearrange("(h p) e -> p h e", p=P))
+        ww = w_words.bitcast(I32).rearrange("e a p n -> p (e a) n")
+        wsc = w_scales.bitcast(I32).rearrange("e a q n -> q (e a) n")
+        for q in range(4):
+            nc.sync.dma_start(out=ws[32 * q : 32 * q + 4, :, :].bitcast(I32), in_=wsc[4 * q : 4 * q + 4])
+
+        def gather(dst, window, s0, n):
+            nc.vector.tensor_copy(dst, window[:].indirect(offsets[:, s0 // 16 : (s0 + n) // 16]))
+
+        wt = {}
+        for i, (a, c0, w, v) in enumerate(CHUNKS):
+            g = held.tile([P, w, 4], BF16, name=f"grp{i}", align_bytes=64)
+            if v < w:
+                nc.scalar.copy(
+                    out=g[:, v:w, :].rearrange("p (c i) j -> p c j i", i=4),
+                    in_=raw[i][:, :, v:w].rearrange("p j (c i) -> p c j i", i=4),
+                )
+            if v > 0:
+                nc.vector.tensor_copy(out=g[:, 0:v, :], in_=raw[i][:, :, 0:v].rearrange("p j w -> p w j"))
+            nc.vector.quantize_mx(
+                out=codes[a][:, c0 : c0 + w].bitcast(FP8X4),
+                scales=plane[4 * a : P, c0 : c0 + w],
+                in_=g[:].rearrange("p w j -> p (w j)"),
+            )
+            for k, n in enumerate(BLOCKS):
+                if GATE[k] == i:
+                    wt[k] = held.tile([P, n * PASSES, 2 * N], U8, name=f"wt{k}", tag=f"raw{i}", align_bytes=64)
+                    g0 = 3 * STARTS[k]
+                    nc.scalar.dma_start(out=wt[k][:].bitcast(I32), in_=ww[:, g0 : g0 + 3 * n, :])
+        for k, n in enumerate(BLOCKS):
+            gather(sp[k][0][:], plane, C * STARTS[k], C * n)
+            for a in (1, 2):
+                nc.sync.dma_start(out=sp[k][a][0:112, :].bitcast(I32), in_=sp[k][0][4 * a : 112 + 4 * a, :].bitcast(I32))
+        gw = {}
+        for a, k, s0, n in WORDS:
+            if (a, k) not in gw:
+                gw[a, k] = held.tile(
+                    [P, C * BLOCKS[k]], U32, name=f"gw{a}_{k}", tag="grp6" if (a, k) in LATE else f"gw{a}_{k}", align_bytes=64
+                )
+            gather(gw[a, k][:, s0 : s0 + n], codes[a], C * STARTS[k] + s0, n)
+
+        def multiply(acc, e, h, a):
+            k = block_of[e]
+            i = e - STARTS[k]
+            nc.tensor.matmul_mx(
+                out=acc[:],
+                lhsT=wt[k][:, 3 * i + a, 256 * h : 256 * h + 256].bitcast(FP4X4),
+                lhsT_scale=ws[:, 3 * e + a, 128 * h : 128 * h + 128],
+                rhs=gw[a, k][:, C * i : C * i + C].bitcast(FP8X4),
+                rhs_scale=sp[k][a][:, C * i : C * i + C],
+                start=(a == 0),
+                stop=(a == PASSES - 1),
+            )
+
+        accs = {}
+        for e in range(LEAD):
+            for h in range(2):
+                accs[e, h] = psum.tile([P, C], F32, name="acc")
+        for a in range(2):
+            for e in range(LEAD):
+                for h in range(2):
+                    multiply(accs[e, h], e, h, a)
+        ov = out.rearrange("(h p) (m s) -> h p m s", p=P, m=2)
+        bounds = [sum(STORE_CUTS[:i]) for i in range(len(STORE_CUTS) + 1)]
+        for lo, hi in zip(bounds[:-1], bounds[1:]):
+            for e in range(lo, hi):
+                for h in range(2):
+                    if e < LEAD:
+                        acc = accs[e, h]
+                        multiply(acc, e, h, 2)
+                    else:
+                        acc = psum.tile([P, C], F32, name="acc")
+                        for a in range(PASSES):
+                            multiply(acc, e, h, a)
+                    nc.scalar.activation(
+                        out=ot[:, h, :, e, :], in_=acc[:].rearrange("p (m u) -> p m u", m=2), func=RELU, bias=bias[:, h, e : e + 1]
+                    )
+            for h, queue in ((0, nc.sync), (1, nc.sync)):
+                queue.dma_start(
+                    out=ov[h, :, :, 64 * lo : 64 * hi], in_=ot[:, h, :, lo:hi, :].rearrange("p m e u -> p m (e u)")
+                )

@@ -16,13 +16,15 @@ FP8X4 = mybir.dt.float8_e4m3fn_x4
 FP4X4 = mybir.dt.float4_e2m1fn_x4
 RELU = mybir.ActivationFunctionType.Relu
 
-CHUNKS = [(0, 0, 512, 288), (0, 512, 256, 144), (0, 768, 256, 144), (1, 0, 512, 0), (1, 512, 512, 0), (2, 0, 512, 0), (2, 512, 512, 192)]
+CHUNKS = [(0, 0, 512, 288), (0, 512, 256, 144), (0, 768, 256, 144), (1, 0, 512, 128), (1, 512, 512, 192), (2, 0, 512, 128), (2, 512, 512, 288)]
 WORDS = [(0, 0, 0, 512), (0, 1, 0, 512), (0, 2, 0, 512), (1, 0, 0, 512), (1, 1, 0, 512), (2, 0, 0, 512), (2, 1, 0, 512), (1, 2, 0, 512), (2, 2, 0, 256), (2, 2, 256, 256)]
 LATE = [(1, 2)]
 BLOCKS = [4,4,4]
 STARTS = [sum(BLOCKS[:k]) for k in range(len(BLOCKS))]
 STORE_CUTS = [4,4,2,2]
-GATE = [4,5,6]
+V_EVAC = 10
+ADD = mybir.AluOpType.add
+MAX = mybir.AluOpType.max
 LEAD = 4
 
 
@@ -43,38 +45,34 @@ def tile_moe_eps_lin_relu_kernel(tc, xT, w_words, w_scales, b, offs, out):
             [held.tile([P, n * C], U8, name=f"sp{k}_{a}", align_bytes=64) for a in range(PASSES)] for k, n in enumerate(BLOCKS)
         ]
         warm = held.tile([P, 1], F32, name="warm")
-        nc.gpsimd.memset(warm[:], 0)
+        nc.vector.memset(warm[:], 0)
         nc.scalar.activation(out=warm[:], in_=warm[:], func=RELU)
-        nc.gpsimd.memset(plane[:].bitcast(I32), 0)
-        nc.gpsimd.memset(ws[:].rearrange("p g n -> p (g n)").bitcast(I32), 0)
+        nc.vector.memset(ws[:].rearrange("p g n -> p (g n)").bitcast(I32), 0)
+        nc.vector.memset(plane[:].bitcast(I32), 0)
         for k in range(len(BLOCKS)):
             for a in (1, 2):
-                nc.gpsimd.memset(sp[k][a][:].bitcast(I32), 0)
+                nc.vector.memset(sp[k][a][:].bitcast(I32), 0)
 
+        ww = w_words.bitcast(I32).rearrange("e a p n -> p (e a) n")
+        wsc = w_scales.bitcast(I32).rearrange("e a q n -> q (e a) n")
+        for r in range(4):
+            nc.gpsimd.dma_start(out=ws[r:P:32, :, :].bitcast(I32), in_=wsc[r:16:4])
         raw = []
         for i, (a, c0, w, v) in enumerate(CHUNKS):
             r = held.tile([P, 4, w], F32, name=f"raw{i}", align_bytes=64)
             nc.sync.dma_start(out=r[:], in_=xT[512 * a : 512 * a + 512, c0 : c0 + w].rearrange("(p j) w -> p j w", j=4))
             raw.append(r)
-            if i == 1:
+            if i == 0:
                 nc.sync.dma_start(offsets[:], offs)
-                nc.sync.dma_start(out=bias[:], in_=b.rearrange("(h p) e -> p h e", p=P))
-        ww = w_words.bitcast(I32).rearrange("e a p n -> p (e a) n")
-        wsc = w_scales.bitcast(I32).rearrange("e a q n -> q (e a) n")
-        for q in range(4):
-            nc.sync.dma_start(out=ws[32 * q : 32 * q + 4, :, :].bitcast(I32), in_=wsc[4 * q : 4 * q + 4])
+                nc.scalar.dma_start(out=bias[:], in_=b.rearrange("(h p) e -> p h e", p=P))
 
         def gather(dst, window, s0, n):
             nc.vector.tensor_copy(dst, window[:].indirect(offsets[:, s0 // 16 : (s0 + n) // 16]))
 
-        wt = {}
         for i, (a, c0, w, v) in enumerate(CHUNKS):
             g = held.tile([P, w, 4], BF16, name=f"grp{i}", align_bytes=64)
             if v < w:
-                nc.scalar.copy(
-                    out=g[:, v:w, :].rearrange("p (c i) j -> p c j i", i=4),
-                    in_=raw[i][:, :, v:w].rearrange("p j (c i) -> p c j i", i=4),
-                )
+                nc.scalar.copy(out=g[:, v:w, :], in_=raw[i][:, :, v:w].rearrange("p j w -> p w j"))
             if v > 0:
                 nc.vector.tensor_copy(out=g[:, 0:v, :], in_=raw[i][:, :, 0:v].rearrange("p j w -> p w j"))
             nc.vector.quantize_mx(
@@ -82,11 +80,15 @@ def tile_moe_eps_lin_relu_kernel(tc, xT, w_words, w_scales, b, offs, out):
                 scales=plane[4 * a : P, c0 : c0 + w],
                 in_=g[:].rearrange("p w j -> p (w j)"),
             )
-            for k, n in enumerate(BLOCKS):
-                if GATE[k] == i:
-                    wt[k] = held.tile([P, n * PASSES, 2 * N], U8, name=f"wt{k}", tag=f"raw{i}", align_bytes=64)
-                    g0 = 3 * STARTS[k]
-                    nc.scalar.dma_start(out=wt[k][:].bitcast(I32), in_=ww[:, g0 : g0 + 3 * n, :])
+        n0 = 3 * BLOCKS[0]
+        wt0 = held.tile([P, n0, 2 * N], U8, name="wt0", tag="raw5", align_bytes=64)
+        wt1 = held.tile([P, E * PASSES - n0, 2 * N], U8, name="wt1", tag="raw6", align_bytes=64)
+        wt = []
+        for k, n in enumerate(BLOCKS):
+            g0 = 3 * STARTS[k]
+            part = wt1[:, g0 - n0 : g0 - n0 + 3 * n, :] if k else wt0[:]
+            nc.scalar.dma_start(out=part.bitcast(I32), in_=ww[:, g0 : g0 + 3 * n, :])
+            wt.append(part)
         for k, n in enumerate(BLOCKS):
             gather(sp[k][0][:], plane, C * STARTS[k], C * n)
             for a in (1, 2):
@@ -95,7 +97,7 @@ def tile_moe_eps_lin_relu_kernel(tc, xT, w_words, w_scales, b, offs, out):
         for a, k, s0, n in WORDS:
             if (a, k) not in gw:
                 gw[a, k] = held.tile(
-                    [P, C * BLOCKS[k]], U32, name=f"gw{a}_{k}", tag="grp6" if (a, k) in LATE else f"gw{a}_{k}", align_bytes=64
+                    [P, C * BLOCKS[k]], U32, name=f"gw{a}_{k}", tag="grp5" if (a, k) in LATE else f"gw{a}_{k}", align_bytes=64
                 )
             gather(gw[a, k][:, s0 : s0 + n], codes[a], C * STARTS[k] + s0, n)
 
@@ -132,10 +134,12 @@ def tile_moe_eps_lin_relu_kernel(tc, xT, w_words, w_scales, b, offs, out):
                         acc = psum.tile([P, C], F32, name="acc")
                         for a in range(PASSES):
                             multiply(acc, e, h, a)
-                    nc.scalar.activation(
-                        out=ot[:, h, :, e, :], in_=acc[:].rearrange("p (m u) -> p m u", m=2), func=RELU, bias=bias[:, h, e : e + 1]
-                    )
-            for h, queue in ((0, nc.sync), (1, nc.sync)):
-                queue.dma_start(
+                    res, sums = ot[:, h, :, e, :], acc[:].rearrange("p (m u) -> p m u", m=2)
+                    if e >= V_EVAC and h == 1:
+                        nc.vector.tensor_scalar(res, sums, bias[:, h, e : e + 1], 0.0, ADD, MAX)
+                    else:
+                        nc.scalar.activation(out=res, in_=sums, func=RELU, bias=bias[:, h, e : e + 1])
+            for h in range(2):
+                nc.sync.dma_start(
                     out=ov[h, :, :, 64 * lo : 64 * hi], in_=ot[:, h, :, lo:hi, :].rearrange("p m e u -> p m (e u)")
                 )

@@ -16,15 +16,16 @@ FP8X4 = mybir.dt.float8_e4m3fn_x4
 FP4X4 = mybir.dt.float4_e2m1fn_x4
 RELU = mybir.ActivationFunctionType.Relu
 
-CHUNKS = [(0, 0, 512, 288), (0, 512, 256, 144), (0, 768, 256, 144), (1, 0, 512, 128), (1, 512, 512, 192), (2, 0, 512, 128), (2, 512, 512, 288)]
+ADD = mybir.AluOpType.add
+MAX = mybir.AluOpType.max
+LOADS = [(0, 0, 512), (0, 512, 512), (1, 0, 1024), (2, 0, 1024)]
+UNITS = [(0, 0, 512, 256), (1, 0, 512, 336), (2, 0, 512, 352), (2, 512, 512, 64), (3, 0, 512, 320), (3, 512, 512, 32)]
 WORDS = [(0, 0, 0, 512), (0, 1, 0, 512), (0, 2, 0, 512), (1, 0, 0, 512), (1, 1, 0, 512), (2, 0, 0, 512), (2, 1, 0, 512), (1, 2, 0, 512), (2, 2, 0, 256), (2, 2, 256, 256)]
-LATE = [(1, 2)]
+LATE = {(1, 2): "grp5"}
 BLOCKS = [4,4,4]
 STARTS = [sum(BLOCKS[:k]) for k in range(len(BLOCKS))]
 STORE_CUTS = [4,4,2,2]
 V_EVAC = 10
-ADD = mybir.AluOpType.add
-MAX = mybir.AluOpType.max
 LEAD = 4
 
 
@@ -41,63 +42,65 @@ def tile_moe_eps_lin_relu_kernel(tc, xT, w_words, w_scales, b, offs, out):
         codes = [held.tile([P, T], U32, name=f"codes{a}", align_bytes=64) for a in range(PASSES)]
         ot = held.tile([P, 2, 2, E, 64], F32, name="ot", align_bytes=64)
         block_of = [k for k, n in enumerate(BLOCKS) for i in range(n)]
+        wt = [held.tile([P, n * PASSES, 2 * N], U8, name=f"wt{k}", align_bytes=64) for k, n in enumerate(BLOCKS[:-1])]
         sp = [
             [held.tile([P, n * C], U8, name=f"sp{k}_{a}", align_bytes=64) for a in range(PASSES)] for k, n in enumerate(BLOCKS)
         ]
         warm = held.tile([P, 1], F32, name="warm")
         nc.vector.memset(warm[:], 0)
         nc.scalar.activation(out=warm[:], in_=warm[:], func=RELU)
-        nc.vector.memset(ws[:].rearrange("p g n -> p (g n)").bitcast(I32), 0)
         nc.vector.memset(plane[:].bitcast(I32), 0)
+        nc.vector.memset(ws[:].rearrange("p g n -> p (g n)").bitcast(I32), 0)
         for k in range(len(BLOCKS)):
             for a in (1, 2):
                 nc.vector.memset(sp[k][a][:].bitcast(I32), 0)
 
-        ww = w_words.bitcast(I32).rearrange("e a p n -> p (e a) n")
-        wsc = w_scales.bitcast(I32).rearrange("e a q n -> q (e a) n")
-        for r in range(4):
-            nc.gpsimd.dma_start(out=ws[r:P:32, :, :].bitcast(I32), in_=wsc[r:16:4])
         raw = []
-        for i, (a, c0, w, v) in enumerate(CHUNKS):
+        for i, (a, c0, w) in enumerate(LOADS):
             r = held.tile([P, 4, w], F32, name=f"raw{i}", align_bytes=64)
             nc.sync.dma_start(out=r[:], in_=xT[512 * a : 512 * a + 512, c0 : c0 + w].rearrange("(p j) w -> p j w", j=4))
             raw.append(r)
-            if i == 0:
+            if i == 1:
                 nc.sync.dma_start(offsets[:], offs)
-                nc.scalar.dma_start(out=bias[:], in_=b.rearrange("(h p) e -> p h e", p=P))
+        ww = w_words.bitcast(I32).rearrange("e a p n -> p (e a) n")
+        wsc = w_scales.bitcast(I32).rearrange("e a q n -> q (e a) n")
+        for r in range(4):
+            nc.sync.dma_start(out=ws[r:P:32, :, :].bitcast(I32), in_=wsc[r:16:4])
+        def load_weights(k):
+            g0 = 3 * STARTS[k]
+            nc.sync.dma_start(out=wt[k][:].bitcast(I32), in_=ww[:, g0 : g0 + 3 * BLOCKS[k], :])
+
+        for k in range(len(BLOCKS) - 1):
+            load_weights(k)
+        nc.sync.dma_start(out=bias[:], in_=b.rearrange("(h p) e -> p h e", p=P))
 
         def gather(dst, window, s0, n):
             nc.vector.tensor_copy(dst, window[:].indirect(offsets[:, s0 // 16 : (s0 + n) // 16]))
 
-        for i, (a, c0, w, v) in enumerate(CHUNKS):
+        for i, (load, off, w, v) in enumerate(UNITS):
+            a, c0 = LOADS[load][0], LOADS[load][1] + off
             g = held.tile([P, w, 4], BF16, name=f"grp{i}", align_bytes=64)
+            src = raw[load][:].rearrange("p j w -> p w j")
             if v < w:
-                nc.scalar.copy(out=g[:, v:w, :], in_=raw[i][:, :, v:w].rearrange("p j w -> p w j"))
+                nc.scalar.copy(out=g[:, v:w, :], in_=src[:, off + v : off + w, :])
             if v > 0:
-                nc.vector.tensor_copy(out=g[:, 0:v, :], in_=raw[i][:, :, 0:v].rearrange("p j w -> p w j"))
+                nc.vector.tensor_copy(out=g[:, 0:v, :], in_=src[:, off : off + v, :])
             nc.vector.quantize_mx(
                 out=codes[a][:, c0 : c0 + w].bitcast(FP8X4),
                 scales=plane[4 * a : P, c0 : c0 + w],
                 in_=g[:].rearrange("p w j -> p (w j)"),
             )
-        n0 = 3 * BLOCKS[0]
-        wt0 = held.tile([P, n0, 2 * N], U8, name="wt0", tag="raw5", align_bytes=64)
-        wt1 = held.tile([P, E * PASSES - n0, 2 * N], U8, name="wt1", tag="raw6", align_bytes=64)
-        wt = []
-        for k, n in enumerate(BLOCKS):
-            g0 = 3 * STARTS[k]
-            part = wt1[:, g0 - n0 : g0 - n0 + 3 * n, :] if k else wt0[:]
-            nc.scalar.dma_start(out=part.bitcast(I32), in_=ww[:, g0 : g0 + 3 * n, :])
-            wt.append(part)
         for k, n in enumerate(BLOCKS):
             gather(sp[k][0][:], plane, C * STARTS[k], C * n)
             for a in (1, 2):
                 nc.sync.dma_start(out=sp[k][a][0:112, :].bitcast(I32), in_=sp[k][0][4 * a : 112 + 4 * a, :].bitcast(I32))
+        wt.append(held.tile([P, BLOCKS[-1] * PASSES, 2 * N], U8, name="wt_last", tag="plane", align_bytes=64))
+        load_weights(len(BLOCKS) - 1)
         gw = {}
         for a, k, s0, n in WORDS:
             if (a, k) not in gw:
                 gw[a, k] = held.tile(
-                    [P, C * BLOCKS[k]], U32, name=f"gw{a}_{k}", tag="grp5" if (a, k) in LATE else f"gw{a}_{k}", align_bytes=64
+                    [P, C * BLOCKS[k]], U32, name=f"gw{a}_{k}", tag=LATE.get((a, k), f"gw{a}_{k}"), align_bytes=64
                 )
             gather(gw[a, k][:, s0 : s0 + n], codes[a], C * STARTS[k] + s0, n)
 

import concourse.mybir as mybir

FLOPS = 2 * 1536 * 1536 * 256

K, T, E, C, N = 1536, 1024, 12, 128, 256
P = 128
PASSES = 3
S = E * C
F32 = mybir.dt.float32
BF16 = mybir.dt.bfloat16
I32 = mybir.dt.int32
U32 = mybir.dt.uint32
U16 = mybir.dt.uint16
U8 = mybir.dt.uint8
FP8X4 = mybir.dt.float8_e4m3fn_x4
FP4X4 = mybir.dt.float4_e2m1fn_x4
RELU = mybir.ActivationFunctionType.Relu

ADD = mybir.AluOpType.add
MAX = mybir.AluOpType.max
LOADS = [(0, 0, 512), (0, 512, 512), (1, 0, 1024), (2, 0, 1024)]
UNITS = [(0, 0, 512, 256), (1, 0, 512, 336), (2, 0, 512, 352), (2, 512, 512, 64), (3, 0, 512, 320), (3, 512, 512, 32)]
WORDS = [(0, 0, 0, 512), (0, 1, 0, 512), (0, 2, 0, 512), (1, 0, 0, 512), (1, 1, 0, 512), (2, 0, 0, 512), (2, 1, 0, 512), (1, 2, 0, 512), (2, 2, 0, 256), (2, 2, 256, 256)]
LATE = {(1, 2): "grp5"}
BLOCKS = [4,4,4]
STARTS = [sum(BLOCKS[:k]) for k in range(len(BLOCKS))]
STORE_CUTS = [4,4,2,2]
V_EVAC = 10
LEAD = 4


def tile_moe_eps_lin_relu_kernel(tc, xT, w_words, w_scales, b, offs, out):
    nc = tc.nc
    with (
        tc.tile_pool(name="held", bufs=1) as held,
        tc.psum_pool(name="psum", bufs=8) as psum,
    ):
        offsets = held.tile([P, S // 16], U16, name="offsets")
        bias = held.tile([P, 2, E], F32, name="bias")
        ws = held.tile([P, E * PASSES, N], U8, name="ws", align_bytes=64)
        plane = held.tile([P, T], U8, name="plane", align_bytes=64)
        codes = [held.tile([P, T], U32, name=f"codes{a}", align_bytes=64) for a in range(PASSES)]
        ot = held.tile([P, 2, 2, E, 64], F32, name="ot", align_bytes=64)
        block_of = [k for k, n in enumerate(BLOCKS) for i in range(n)]
        wt = [held.tile([P, n * PASSES, 2 * N], U8, name=f"wt{k}", align_bytes=64) for k, n in enumerate(BLOCKS[:-1])]
        sp = [
            [held.tile([P, n * C], U8, name=f"sp{k}_{a}", align_bytes=64) for a in range(PASSES)] for k, n in enumerate(BLOCKS)
        ]
        warm = held.tile([P, 1], F32, name="warm")
        nc.vector.memset(warm[:], 0)
        nc.scalar.activation(out=warm[:], in_=warm[:], func=RELU)
        nc.vector.memset(plane[:].bitcast(I32), 0)
        nc.vector.memset(ws[:].rearrange("p g n -> p (g n)").bitcast(I32), 0)
        for k in range(len(BLOCKS)):
            for a in (1, 2):
                nc.vector.memset(sp[k][a][:].bitcast(I32), 0)

        raw = []
        for i, (a, c0, w) in enumerate(LOADS):
            r = held.tile([P, 4, w], F32, name=f"raw{i}", align_bytes=64)
            nc.sync.dma_start(out=r[:], in_=xT[512 * a : 512 * a + 512, c0 : c0 + w].rearrange("(p j) w -> p j w", j=4))
            raw.append(r)
            if i == 1:
                nc.sync.dma_start(offsets[:], offs)
        ww = w_words.bitcast(I32).rearrange("e a p n -> p (e a) n")
        wsc = w_scales.bitcast(I32).rearrange("e a q n -> q (e a) n")
        for r in range(4):
            nc.sync.dma_start(out=ws[r:P:32, :, :].bitcast(I32), in_=wsc[r:16:4])
        def load_weights(k):
            g0 = 3 * STARTS[k]
            nc.sync.dma_start(out=wt[k][:].bitcast(I32), in_=ww[:, g0 : g0 + 3 * BLOCKS[k], :])

        for k in range(len(BLOCKS) - 1):
            load_weights(k)
        nc.sync.dma_start(out=bias[:], in_=b.rearrange("(h p) e -> p h e", p=P))

        def gather(dst, window, s0, n):
            nc.vector.tensor_copy(dst, window[:].indirect(offsets[:, s0 // 16 : (s0 + n) // 16]))

        for i, (load, off, w, v) in enumerate(UNITS):
            a, c0 = LOADS[load][0], LOADS[load][1] + off
            g = held.tile([P, w, 4], BF16, name=f"grp{i}", align_bytes=64)
            src = raw[load][:].rearrange("p j w -> p w j")
            if v < w:
                nc.scalar.copy(out=g[:, v:w, :], in_=src[:, off + v : off + w, :])
            if v > 0:
                nc.vector.tensor_copy(out=g[:, 0:v, :], in_=src[:, off : off + v, :])
            nc.vector.quantize_mx(
                out=codes[a][:, c0 : c0 + w].bitcast(FP8X4),
                scales=plane[4 * a : P, c0 : c0 + w],
                in_=g[:].rearrange("p w j -> p (w j)"),
            )
        for k, n in enumerate(BLOCKS):
            gather(sp[k][0][:], plane, C * STARTS[k], C * n)
            for a in (1, 2):
                nc.sync.dma_start(out=sp[k][a][0:112, :].bitcast(I32), in_=sp[k][0][4 * a : 112 + 4 * a, :].bitcast(I32))
        wt.append(held.tile([P, BLOCKS[-1] * PASSES, 2 * N], U8, name="wt_last", tag="plane", align_bytes=64))
        load_weights(len(BLOCKS) - 1)
        gw = {}
        for a, k, s0, n in WORDS:
            if (a, k) not in gw:
                gw[a, k] = held.tile(
                    [P, C * BLOCKS[k]], U32, name=f"gw{a}_{k}", tag=LATE.get((a, k), f"gw{a}_{k}"), align_bytes=64
                )
            gather(gw[a, k][:, s0 : s0 + n], codes[a], C * STARTS[k] + s0, n)

        def multiply(acc, e, h, a):
            k = block_of[e]
            i = e - STARTS[k]
            nc.tensor.matmul_mx(
                out=acc[:],
                lhsT=wt[k][:, 3 * i + a, 256 * h : 256 * h + 256].bitcast(FP4X4),
                lhsT_scale=ws[:, 3 * e + a, 128 * h : 128 * h + 128],
                rhs=gw[a, k][:, C * i : C * i + C].bitcast(FP8X4),
                rhs_scale=sp[k][a][:, C * i : C * i + C],
                start=(a == 0),
                stop=(a == PASSES - 1),
            )

        accs = {}
        for e in range(LEAD):
            for h in range(2):
                accs[e, h] = psum.tile([P, C], F32, name="acc")
        for a in range(2):
            for e in range(LEAD):
                for h in range(2):
                    multiply(accs[e, h], e, h, a)
        ov = out.rearrange("(h p) (m s) -> h p m s", p=P, m=2)
        bounds = [sum(STORE_CUTS[:i]) for i in range(len(STORE_CUTS) + 1)]
        for lo, hi in zip(bounds[:-1], bounds[1:]):
            for e in range(lo, hi):
                for h in range(2):
                    if e < LEAD:
                        acc = accs[e, h]
                        multiply(acc, e, h, 2)
                    else:
                        acc = psum.tile([P, C], F32, name="acc")
                        for a in range(PASSES):
                            multiply(acc, e, h, a)
                    res, sums = ot[:, h, :, e, :], acc[:].rearrange("p (m u) -> p m u", m=2)
                    if e >= V_EVAC and h == 1:
                        nc.vector.tensor_scalar(res, sums, bias[:, h, e : e + 1], 0.0, ADD, MAX)
                    else:
                        nc.scalar.activation(out=res, in_=sums, func=RELU, bias=bias[:, h, e : e + 1])
            for h in range(2):
                nc.sync.dma_start(
                    out=ov[h, :, :, 64 * lo : 64 * hi], in_=ot[:, h, :, lo:hi, :].rearrange("p m e u -> p m (e u)")
                )
